import numpy as np
import ml_dtypes

BF16 = ml_dtypes.bfloat16


def bf(x):
    return np.asarray(x, np.float32).astype(BF16)


def f32(x):
    return np.asarray(x, np.float32)


def f64(x):
    return np.asarray(x).astype(np.float64)


def striped(idx):
    return np.tile(idx.reshape(-1, 16).T, (8, 1))


S, K, M, N, E, Q = 1024, 256, 128, 2048, 8, 256


def gelu_tanh(v):
    return 0.5 * v * (1.0 + np.tanh(np.sqrt(2.0 / np.pi) * (v + 0.044715 * v**3)))


def two_experts():
    first = np.random.permutation(S).reshape(E, S // E)
    return np.concatenate([np.random.permutation(np.concatenate([first[e], first[(e + 1) % E]])) for e in range(E)])


def setup_inputs():
    return {"table": bf(np.random.standard_normal((K, S))), "w": bf(np.random.standard_normal((E, K, M)) / np.sqrt(K)), "b": f32(0.5 * np.random.standard_normal((M, 1))), "offs": striped(two_experts())}


def reference(table, w, b, offs):
    idx = offs[:16].T.reshape(-1)
    x = f64(table)[:, idx]
    y = np.concatenate([f64(w)[e].T @ x[:, e * Q : (e + 1) * Q] for e in range(E)], axis=1)
    return gelu_tanh(y + f64(b))

@@ -1,0 +1,47 @@
+import concourse.mybir as mybir
+
+P = 128
+S, K, M = 1024, 256, 128
+E, Q = 8, 256
+N = E * Q
+C = K // P
+L = Q // 16
+FLOPS = 2 * K * M * N
+
+BF16, F32, U16 = mybir.dt.bfloat16, mybir.dt.float32, mybir.dt.uint16
+GELU = mybir.ActivationFunctionType.Gelu_apprx_tanh
+
+
+def tile_gather_matmul_kernel(tc, table, w, b, offs, out):
+    nc = tc.nc
+    with (
+        tc.tile_pool(name="held", bufs=1) as held,
+        tc.tile_pool(name="results", bufs=E) as results,
+        tc.psum_pool(name="sums", bufs=E) as sums,
+    ):
+        offsets = held.tile([P, N // 16], U16, name="offsets")
+        nc.sync.dma_start(offsets[:], offs)
+        table_rows = table.rearrange("(p c) s -> c p s", c=C)
+        blocks = []
+        for c in range(C):
+            block = held.tile([P, S], BF16, name=f"block{c}")
+            nc.sync.dma_start(block[:], table_rows[c])
+            blocks.append(block)
+        weights = held.tile([P, E, C, M], BF16, name="weights")
+        nc.scalar.dma_start(weights[:], w.rearrange("e (p c) m -> p e c m", c=C))
+        bias = held.tile([P, 1], F32, name="bias")
+        nc.scalar.dma_start(bias[:], b)
+
+        for e in range(E):
+            total = sums.tile([P, Q], F32, name="total")
+            for c in range(C):
+                nc.tensor.matmul(
+                    total[:],
+                    weights[:, e, c, :],
+                    blocks[c][:].indirect(offsets[:, e * L : (e + 1) * L]),
+                    start=c == 0,
+                    stop=c == C - 1,
+                )
+            result = results.tile([P, Q], F32, name="result")
+            nc.scalar.activation(result[:], total[:], GELU, bias=bias[:])
+            nc.sync.dma_start(out[:, e * Q : (e + 1) * Q], result[:])

@@ -5,6 +5,7 @@ S, K, M = 1024, 256, 128
 E, Q = 8, 256
 N = E * Q
 C = K // P
+PAIR = 2
 L = Q // 16
 FLOPS = 2 * K * M * N
 
@@ -20,24 +21,29 @@ def tile_gather_matmul_kernel(tc, table, w, b, offs, out):
         tc.psum_pool(name="sums", bufs=E) as sums,
     ):
         offsets = held.tile([P, N // 16], U16, name="offsets")
-        nc.sync.dma_start(offsets[:], offs)
-        table_rows = table.rearrange("(p c) s -> c p s", c=C)
-        blocks = []
-        for c in range(C):
-            block = held.tile([P, S], BF16, name=f"block{c}")
-            nc.sync.dma_start(block[:], table_rows[c])
-            blocks.append(block)
-        weights = held.tile([P, E, C, M], BF16, name="weights")
-        nc.scalar.dma_start(weights[:], w.rearrange("e (p c) m -> p e c m", c=C))
+        blocks = [held.tile([P, S], BF16, name=f"block{c}") for c in range(C)]
+        weights = [held.tile([P, PAIR, C, M], BF16, name=f"weights{h}") for h in range(E // PAIR)]
         bias = held.tile([P, 1], F32, name="bias")
+        table_rows = table.rearrange("(p c) s -> c p s", c=C)
+        weight_rows = w.rearrange("(h e) (p c) m -> h p e c m", e=PAIR, c=C)
+        nc.sync.dma_start(offsets[:], offs)
+        nc.sync.dma_start(blocks[0][:], table_rows[0])
+        nc.sync.dma_start(weights[0][:], weight_rows[0])
+        nc.sync.dma_start(blocks[1][:], table_rows[1])
+        for h in range(1, E // PAIR):
+            nc.sync.dma_start(weights[h][:], weight_rows[h])
         nc.scalar.dma_start(bias[:], b)
+        zeros = held.tile([P, 1], F32, name="zeros")
+        nc.vector.memset(zeros[:], 0.0)
+        warmed = held.tile([P, 1], F32, name="warmed")
+        nc.scalar.activation(warmed[:], zeros[:], GELU)
 
         for e in range(E):
             total = sums.tile([P, Q], F32, name="total")
             for c in range(C):
                 nc.tensor.matmul(
                     total[:],
-                    weights[:, e, c, :],
+                    weights[e // PAIR][:, e % PAIR, c, :],
                     blocks[c][:].indirect(offsets[:, e * L : (e + 1) * L]),
                     start=c == 0,
                     stop=c == C - 1,

@@ -28,10 +28,11 @@ def tile_gather_matmul_kernel(tc, table, w, b, offs, out):
         weight_rows = w.rearrange("(h e) (p c) m -> h p e c m", e=PAIR, c=C)
         nc.sync.dma_start(offsets[:], offs)
         nc.sync.dma_start(blocks[0][:], table_rows[0])
-        nc.sync.dma_start(weights[0][:], weight_rows[0])
-        nc.sync.dma_start(blocks[1][:], table_rows[1])
+        nc.scalar.dma_start(weights[0][:], weight_rows[0])
+        nc.scalar.dma_start(blocks[1][:], table_rows[1])
         for h in range(1, E // PAIR):
-            nc.sync.dma_start(weights[h][:], weight_rows[h])
+            queue = nc.sync if h % 2 == 1 else nc.scalar
+            queue.dma_start(weights[h][:], weight_rows[h])
         nc.scalar.dma_start(bias[:], b)
         zeros = held.tile([P, 1], F32, name="zeros")
         nc.vector.memset(zeros[:], 0.0)

import concourse.mybir as mybir

P = 128
S, K, M = 1024, 256, 128
E, Q = 8, 256
N = E * Q
C = K // P
PAIR = 2
L = Q // 16
FLOPS = 2 * K * M * N

BF16, F32, U16 = mybir.dt.bfloat16, mybir.dt.float32, mybir.dt.uint16
GELU = mybir.ActivationFunctionType.Gelu_apprx_tanh


def tile_gather_matmul_kernel(tc, table, w, b, offs, out):
    nc = tc.nc
    with (
        tc.tile_pool(name="held", bufs=1) as held,
        tc.tile_pool(name="results", bufs=E) as results,
        tc.psum_pool(name="sums", bufs=E) as sums,
    ):
        offsets = held.tile([P, N // 16], U16, name="offsets")
        blocks = [held.tile([P, S], BF16, name=f"block{c}") for c in range(C)]
        weights = [held.tile([P, PAIR, C, M], BF16, name=f"weights{h}") for h in range(E // PAIR)]
        bias = held.tile([P, 1], F32, name="bias")
        table_rows = table.rearrange("(p c) s -> c p s", c=C)
        weight_rows = w.rearrange("(h e) (p c) m -> h p e c m", e=PAIR, c=C)
        nc.sync.dma_start(offsets[:], offs)
        nc.sync.dma_start(blocks[0][:], table_rows[0])
        nc.scalar.dma_start(weights[0][:], weight_rows[0])
        nc.scalar.dma_start(blocks[1][:], table_rows[1])
        for h in range(1, E // PAIR):
            queue = nc.sync if h % 2 == 1 else nc.scalar
            queue.dma_start(weights[h][:], weight_rows[h])
        nc.scalar.dma_start(bias[:], b)
        zeros = held.tile([P, 1], F32, name="zeros")
        nc.vector.memset(zeros[:], 0.0)
        warmed = held.tile([P, 1], F32, name="warmed")
        nc.scalar.activation(warmed[:], zeros[:], GELU)

        for e in range(E):
            total = sums.tile([P, Q], F32, name="total")
            for c in range(C):
                nc.tensor.matmul(
                    total[:],
                    weights[e // PAIR][:, e % PAIR, c, :],
                    blocks[c][:].indirect(offsets[:, e * L : (e + 1) * L]),
                    start=c == 0,
                    stop=c == C - 1,
                )
            result = results.tile([P, Q], F32, name="result")
            nc.scalar.activation(result[:], total[:], GELU, bias=bias[:])
            nc.sync.dma_start(out[:, e * Q : (e + 1) * Q], result[:])
